import numpy as np
import ml_dtypes


def mxq(x, axis, fmt="e4m3"):
    dtype, down = {"e4m3": (ml_dtypes.float8_e4m3fn, 7), "e5m2": (ml_dtypes.float8_e5m2, 14)}[fmt]
    v = np.moveaxis(np.asarray(x, np.float32).astype(ml_dtypes.bfloat16).astype(np.float64), axis, -1)
    blocks = v.reshape(v.shape[:-1] + (-1, 32))
    amax = np.abs(blocks).max(-1, keepdims=True)
    byte = np.maximum(np.where(amax > 0, np.frexp(amax)[1] - 1 + 127, 0) - down, 1)
    scale = np.exp2(byte - 127.0)
    codes = (blocks / scale).astype(np.float32).astype(dtype).astype(np.float64)
    return np.moveaxis((codes * scale).reshape(v.shape), -1, axis)


WIDE = False


def mx_kscale(k):
    if not WIDE:
        return np.ones(k)
    levels = np.array([10, -10, 5, -5, 0])
    if k % 512:
        return np.exp2(np.random.permutation(np.resize(levels, k // 32))).repeat(32)
    a = np.empty((k // 512, 16))
    for p in range(k // 512):
        a[p, :8] = np.random.permutation(np.resize(levels, 8))
        for g in range(8):
            far = levels[np.abs(levels - a[p, g]) >= 10]
            a[p, g + 8] = far[np.random.randint(len(far))]
    return np.exp2(a.ravel()).repeat(32)


BF16 = ml_dtypes.bfloat16


def bf(x):
    return np.asarray(x, np.float32).astype(BF16)


def f64(x):
    return np.asarray(x).astype(np.float64)

def planes(Y):
    n, m = Y.shape
    b = f64(bf(Y)).reshape(n // 32, 32, m)
    amax = np.abs(b).max(1)
    byte = np.clip(np.where(amax > 0, np.frexp(amax)[1] - 1 + 127 - 7, 1), 1, 254)
    codes = (b * np.exp2(127.0 - byte)[:, None, :]).reshape(n, m).astype(np.float32).astype(ml_dtypes.float8_e4m3fn).view(np.uint8)
    words = codes.reshape(n // 512, 128, 4, m).transpose(0, 1, 3, 2)
    return np.ascontiguousarray(words), np.ascontiguousarray(byte.astype(np.uint8).reshape(n // 512, 16, m))


I, S, W, C = 4, 512, 1536, 1024

CENTER_STD = 0.3
GAIN_STD = 0.1
LOG_SPREAD = 0.7


def setup_inputs():
    s = mx_kscale(W)
    spectra = np.random.randn(I, S, W) * s
    loadings = np.random.randn(W, C) / np.sqrt(W) / s[:, None]
    gains = 1.0 + GAIN_STD * np.random.randn(I, S)
    centers = CENTER_STD * np.random.randn(C, I)
    spreads = np.exp(LOG_SPREAD * np.random.randn(C))
    return {"spectra": bf(spectra), "loadings": bf(loadings), "gains": bf(gains),
            "centers": bf(centers), "spreads": bf(spreads)}


def reference(spectra, loadings, gains, centers, spreads):
    X = f64(spectra).reshape(I * S, W)
    P = f64(loadings)
    T = mxq(P, 0, "e4m3").T @ mxq(X, 1, "e4m3").T
    T = T.reshape(C, I, S)
    y = (T * f64(gains)[None, :, :] - f64(centers)[:, :, None]) / f64(spreads)[:, None, None]
    Y = y.reshape(C, I * S)
    words, scales = planes(Y)
    return y, words, scales

@@ -1,0 +1,239 @@
+from contextlib import ExitStack
+
+import concourse.mybir as mybir
+from concourse.masks import make_identity
+
+I, S, W, C = 4, 512, 1536, 1024
+FLOPS = 2 * C * I * S * W
+
+F32 = mybir.dt.float32
+BF16 = mybir.dt.bfloat16
+U32 = mybir.dt.uint32
+I32 = mybir.dt.int32
+U8 = mybir.dt.uint8
+FP8X4 = mybir.dt.float8_e4m3fn_x4
+ACT = mybir.ActivationFunctionType
+ALU = mybir.AluOpType
+
+P = 128
+PACK = 4
+KP = P * PACK
+PASSES = W // KP
+GROUPS = C // KP
+UNITS = [(0, 0), (1, 0), (0, 1), (1, 1), (2, 0), (2, 1), (3, 0), (3, 1)]
+HALVES = [(c, h) for c in range(PASSES) for h in range(2)]
+P_SPLIT = [3, 2]
+Y_SPLIT = [384, 384, 384, 384, 256, 256, 256, 336]
+
+
+def tile_scaled_spectral_scores_g2_kernel(tc, spectra, loadings, gains, centers, spreads, out_0, out_1, out_2):
+    nc = tc.nc
+    with ExitStack() as ctx:
+        sb = ctx.enter_context(tc.tile_pool(name="sb", bufs=1))
+        ps = ctx.enter_context(tc.psum_pool(name="ps", bufs=1))
+        ctx.enter_context(tc.manual_schedule())
+        turns = {}
+
+        def rotating(pool, kind, depth, shape, dtype, align=None):
+            n = turns.get(kind, 0)
+            turns[kind] = n + 1
+            name = "%s%d" % (kind, n % depth)
+            if align is None:
+                return pool.tile(shape, dtype, name=name, tag=name)
+            return pool.tile(shape, dtype, name=name, tag=name, align_bytes=align)
+
+        ident = sb.tile([P, P], F32)
+        make_identity(nc, ident[:])
+
+        gain_rows = sb.tile([P, 16], BF16)
+        nc.scalar.dma_start(out=gain_rows[:], in_=gains.rearrange("i (p j) -> (i p) j", j=16))
+        cen = sb.tile([P, GROUPS, PACK * I], BF16)
+        nc.scalar.dma_start(out=cen[:], in_=centers.rearrange("(g p t) i -> p g (t i)", g=GROUPS, t=PACK))
+        spr = sb.tile([P, GROUPS, PACK], BF16)
+        nc.scalar.dma_start(out=spr[:], in_=spreads.rearrange("(g p t) -> p g t", g=GROUPS, t=PACK))
+
+        x_raw, p_raw = {}, {}
+
+        def load_x(i, c):
+            x_raw[i, c] = sb.tile([P, 4, KP], BF16, name="x_raw%d%d" % (i, c))
+            nc.sync.dma_start(out=x_raw[i, c][:], in_=spectra[i, :, c * KP:(c + 1) * KP].rearrange("(j p) k -> p j k", p=P))
+
+        def load_p(g, c):
+            p_raw[g, c] = sb.tile([P, PACK, KP], BF16, name="p_raw%d%d" % (g, c))
+            nc.sync.dma_start(out=p_raw[g, c][:], in_=loadings[c * KP:(c + 1) * KP, g * KP:(g + 1) * KP].rearrange("(p j) n -> p j n", j=PACK))
+
+        for c in range(PASSES):
+            load_x(0, c)
+            load_p(0, c)
+        for c in range(PASSES):
+            load_x(1, c)
+        for c in range(PASSES):
+            load_p(1, c)
+        for i in range(2, I):
+            for c in range(PASSES):
+                load_x(i, c)
+
+        gain_all = sb.tile([P, I * S], BF16)
+        gain_words = gain_rows[:].bitcast(F32)
+        gain_out = gain_all[:].bitcast(F32).rearrange("q (n w) -> q n w", w=8)
+        for h in range(2):
+            bank = rotating(ps, "xt", 4, [P, 4, P], F32)
+            for w in range(4):
+                nc.tensor.transpose(bank[:, w, :], gain_words[:, 4 * h + w:4 * h + w + 1].to_broadcast([P, P]), ident[:])
+            nc.vector.tensor_copy(out=gain_out[:, :, 4 * h:4 * h + 4], in_=bank[:].rearrange("q w n -> q n w"))
+
+        neg_cen = sb.tile([P, GROUPS * PACK, I], F32)
+        nc.scalar.activation(out=neg_cen[:].rearrange("p j i -> p (j i)"), in_=cen[:].rearrange("p g f -> p (g f)"), func=ACT.Identity, scale=-1.0)
+        inv = sb.tile([P, GROUPS * PACK], F32)
+        nc.vector.reciprocal(out=inv[:], in_=spr[:].rearrange("p g t -> p (g t)"))
+        shift = sb.tile([P, GROUPS * PACK, I], F32)
+        nc.vector.tensor_tensor(out=shift[:], in0=neg_cen[:], in1=inv[:].unsqueeze(2).to_broadcast([P, GROUPS * PACK, I]), op=ALU.mult)
+
+        x_bank, x_grp, x_codes, x_scales = {}, {}, {}, {}
+        p_grp, p_codes, p_scales = {}, {}, {}
+        acc, y, y_grp = {}, {}, {}
+        y_scales = sb.tile([P, GROUPS, I * S], U8, align_bytes=64)
+
+        def turn_x(i, c, h):
+            words = x_raw[i, c][:].bitcast(F32)
+            x_bank[i, c, h] = rotating(ps, "xt", 4, [P, 2, 2, P], F32)
+            for j in range(2):
+                for u in range(2):
+                    nc.tensor.transpose(x_bank[i, c, h][:, j, u, :], words[:, 2 * h + j, u::2], ident[:])
+
+        def drain_x(i, c, h):
+            if h == 0:
+                x_grp[i, c] = rotating(sb, "x_grp", 3, [P, S * PACK], BF16, 64)
+            dst = x_grp[i, c][:].bitcast(F32)[:, h * 512:(h + 1) * 512].rearrange("p (j r u) -> p j r u", j=2, u=2)
+            nc.scalar.copy(out=dst, in_=x_bank[i, c, h][:].rearrange("p j u r -> p j r u"))
+
+        def quant_x(i, c):
+            x_codes[i, c] = sb.tile([P, S], U32, name="x_codes%d%d" % (i, c), align_bytes=64)
+            x_scales[i, c] = sb.tile([P, S], U8, name="x_scales%d%d" % (i, c), align_bytes=64)
+            nc.vector.quantize_mx(out=x_codes[i, c][:].bitcast(FP8X4), scales=x_scales[i, c][:], in_=x_grp[i, c][:])
+
+        def weave_p(g, c):
+            p_grp[g, c] = rotating(sb, "p_grp", 3, [P, KP * PACK], BF16, 64)
+            dst = p_grp[g, c][:].rearrange("p (t a b j) -> p a t b j", t=PACK, b=2, j=PACK)
+            src = p_raw[g, c][:].rearrange("p j (a b t) -> p a t b j", b=2, t=PACK)
+            cut = P_SPLIT[g]
+            nc.vector.tensor_copy(out=dst[:, :, :cut], in_=src[:, :, :cut])
+            nc.scalar.copy(out=dst[:, :, cut:], in_=src[:, :, cut:])
+
+        def quant_p(g, c):
+            p_codes[g, c] = sb.tile([P, KP], U32, name="p_codes%d%d" % (g, c), align_bytes=64)
+            p_scales[g, c] = sb.tile([P, KP], U8, name="p_scales%d%d" % (g, c), align_bytes=64)
+            nc.vector.quantize_mx(out=p_codes[g, c][:].bitcast(FP8X4), scales=p_scales[g, c][:], in_=p_grp[g, c][:])
+
+        def multiply(k, t, passes):
+            i, g = UNITS[k]
+            if (k, t) not in acc:
+                acc[k, t] = rotating(ps, "acc", 4, [P, S], F32)
+            cols = slice(t * P, (t + 1) * P)
+            for c in passes:
+                nc.tensor.matmul_mx(
+                    out=acc[k, t][:],
+                    lhsT=p_codes[g, c][:, cols].bitcast(FP8X4), lhsT_scale=p_scales[g, c][:, cols],
+                    rhs=x_codes[i, c][:].bitcast(FP8X4), rhs_scale=x_scales[i, c][:],
+                    start=(c == 0), stop=(c == PASSES - 1))
+
+        def gain(k, t):
+            i, g = UNITS[k]
+            if t == 0:
+                y[k] = rotating(sb, "y", 6, [P, PACK, S], F32)
+            nc.vector.tensor_tensor(out=y[k][:, t, :], in0=acc[k, t][:], in1=gain_all[:, i * S:(i + 1) * S], op=ALU.mult)
+
+        def center(k, t):
+            i, g = UNITS[k]
+            j = g * PACK + t
+            nc.scalar.activation(out=y[k][:, t, :], in_=y[k][:, t, :], func=ACT.Identity, scale=inv[:, j:j + 1], bias=shift[:, j, i:i + 1])
+            rows = out_0[g * KP:(g + 1) * KP, i, :].rearrange("(p t) m -> p t m", t=PACK)
+            nc.sync.dma_start(out=rows[:, t, :], in_=y[k][:, t, :])
+
+        def weave_views(k):
+            if k not in y_grp:
+                y_grp[k] = rotating(sb, "y_grp", 2, [P, S * PACK], BF16, 64)
+            dst = y_grp[k][:].rearrange("p (a b t) -> p a t b", b=4, t=PACK)
+            src = y[k][:].rearrange("p t (a b) -> p a t b", b=4)
+            return dst, src, Y_SPLIT[k] // 4
+
+        def weave_y_vector(k):
+            dst, src, cut = weave_views(k)
+            nc.vector.tensor_copy(out=dst[:, :cut], in_=src[:, :cut])
+
+        def weave_y_scalar(k):
+            dst, src, cut = weave_views(k)
+            nc.scalar.copy(out=dst[:, cut:], in_=src[:, cut:])
+
+        def quant_y(k):
+            i, g = UNITS[k]
+            cols = slice(i * S, (i + 1) * S)
+            y_codes = rotating(sb, "y_codes", 4, [P, S], U32, 64)
+            nc.vector.quantize_mx(out=y_codes[:].bitcast(FP8X4), scales=y_scales[:, g, cols], in_=y_grp[k][:])
+            nc.sync.dma_start(out=out_1[g, :, cols, :].rearrange("p m t -> p (m t)").bitcast(I32), in_=y_codes[:].bitcast(I32))
+
+        def store_scales(engine, cols):
+            for q in range(4):
+                engine.dma_start(out=out_2[:, 4 * q:4 * q + 4, cols].rearrange("g r n -> r g n").bitcast(I32),
+                                 in_=y_scales[32 * q:32 * q + 4, :, cols].bitcast(I32))
+
+        def prepare_x(i, c):
+            for h in range(2):
+                turn_x(i, c, h)
+                drain_x(i, c, h)
+
+        every = range(PASSES)
+        for c in every:
+            prepare_x(0, c)
+            if c > 0:
+                for t in range(PACK):
+                    multiply(0, t, [c - 1])
+            weave_p(0, c)
+            quant_x(0, c)
+            quant_p(0, c)
+        prepare_x(1, 0)
+        for t in range(PACK):
+            multiply(0, t, [PASSES - 1])
+        prepare_x(1, 1)
+        prepare_x(1, 2)
+        for t in range(PACK):
+            if t < PASSES:
+                quant_x(1, t)
+            gain(0, t)
+        for t in range(PACK):
+            multiply(1, t, every)
+        for t in range(PACK):
+            center(0, t)
+            if t < PASSES:
+                weave_p(1, t)
+            if t > 0:
+                quant_p(1, t - 1)
+
+        last = len(UNITS) - 1
+        for k in range(1, last + 1):
+            ahead = (k + 3) // 2
+            halves = HALVES[3 * ((k + 1) % 2):3 * ((k + 1) % 2) + 3] if ahead < I else []
+            weave_y_scalar(k - 1)
+            for c, h in halves:
+                turn_x(ahead, c, h)
+            for t in range(PACK):
+                gain(k, t)
+                center(k, t)
+                if t < len(halves):
+                    drain_x(ahead, *halves[t])
+                if k < last:
+                    multiply(k + 1, t, every)
+                if t == (1 if k < last else PACK - 1):
+                    weave_y_vector(k - 1)
+            whole = [c for c, h in halves if h == 1]
+            for c in whole[:1]:
+                quant_x(ahead, c)
+            quant_y(k - 1)
+            for c in whole[1:]:
+                quant_x(ahead, c)
+            if k == last - 1:
+                store_scales(nc.sync, slice(0, (I - 1) * S))
+        weave_y_vector(last)
+        weave_y_scalar(last)
+        quant_y(last)
+        store_scales(nc.scalar, slice((I - 1) * S, I * S))

@@ -22,8 +22,9 @@ PASSES = W // KP
 GROUPS = C // KP
 UNITS = [(0, 0), (1, 0), (0, 1), (1, 1), (2, 0), (2, 1), (3, 0), (3, 1)]
 HALVES = [(c, h) for c in range(PASSES) for h in range(2)]
-P_SPLIT = [3, 2]
-Y_SPLIT = [384, 384, 384, 384, 256, 256, 256, 336]
+P_SPLIT = [[3, 3, 3], [3, 2, 2]]
+CARRY_AT = 1
+Y_SPLIT = [448, 448, 448, 448, 256, 256, 256, 336]
 
 
 def tile_scaled_spectral_scores_g2_kernel(tc, spectra, loadings, gains, centers, spreads, out_0, out_1, out_2):
@@ -65,14 +66,29 @@ def tile_scaled_spectral_scores_g2_kernel(tc, spectra, loadings, gains, centers,
         for c in range(PASSES):
             load_x(0, c)
             load_p(0, c)
-        for c in range(PASSES):
-            load_x(1, c)
-        for c in range(PASSES):
-            load_p(1, c)
+        load_x(1, 0)
+        load_p(1, 0)
+        load_x(1, 1)
+        load_x(1, 2)
+        load_p(1, 1)
+        load_p(1, 2)
         for i in range(2, I):
             for c in range(PASSES):
                 load_x(i, c)
 
+        warm_in = sb.tile([P, 256 * PACK], BF16, align_bytes=64)
+        nc.vector.memset(warm_in[:].bitcast(I32), 0)
+        warm_codes = sb.tile([P, 256], U32, align_bytes=64)
+        warm_scales = sb.tile([P, 256], U8, align_bytes=64)
+        nc.vector.quantize_mx(out=warm_codes[:].bitcast(FP8X4), scales=warm_scales[:], in_=warm_in[:])
+        warm_out = ps.tile([P, S], F32, name="acc3", tag="acc3")
+
+        def warm(n):
+            for rep in range(2 * n):
+                nc.tensor.matmul_mx(out=warm_out[:, :256], lhsT=warm_codes[:, :P].bitcast(FP8X4), lhsT_scale=warm_scales[:, :P],
+                                    rhs=warm_codes[:].bitcast(FP8X4), rhs_scale=warm_scales[:], start=True, stop=True)
+
+        warm(2)
         gain_all = sb.tile([P, I * S], BF16)
         gain_words = gain_rows[:].bitcast(F32)
         gain_out = gain_all[:].bitcast(F32).rearrange("q (n w) -> q n w", w=8)
@@ -103,7 +119,7 @@ def tile_scaled_spectral_scores_g2_kernel(tc, spectra, loadings, gains, centers,
 
         def drain_x(i, c, h):
             if h == 0:
-                x_grp[i, c] = rotating(sb, "x_grp", 3, [P, S * PACK], BF16, 64)
+                x_grp[i, c] = rotating(sb, "x_grp", 4, [P, S * PACK], BF16, 64)
             dst = x_grp[i, c][:].bitcast(F32)[:, h * 512:(h + 1) * 512].rearrange("p (j r u) -> p j r u", j=2, u=2)
             nc.scalar.copy(out=dst, in_=x_bank[i, c, h][:].rearrange("p j u r -> p j r u"))
 
@@ -113,10 +129,10 @@ def tile_scaled_spectral_scores_g2_kernel(tc, spectra, loadings, gains, centers,
             nc.vector.quantize_mx(out=x_codes[i, c][:].bitcast(FP8X4), scales=x_scales[i, c][:], in_=x_grp[i, c][:])
 
         def weave_p(g, c):
-            p_grp[g, c] = rotating(sb, "p_grp", 3, [P, KP * PACK], BF16, 64)
+            p_grp[g, c] = rotating(sb, "p_grp", 4, [P, KP * PACK], BF16, 64)
             dst = p_grp[g, c][:].rearrange("p (t a b j) -> p a t b j", t=PACK, b=2, j=PACK)
             src = p_raw[g, c][:].rearrange("p j (a b t) -> p a t b j", b=2, t=PACK)
-            cut = P_SPLIT[g]
+            cut = P_SPLIT[g][c]
             nc.vector.tensor_copy(out=dst[:, :, :cut], in_=src[:, :, :cut])
             nc.scalar.copy(out=dst[:, :, cut:], in_=src[:, :, cut:])
 
@@ -184,53 +200,97 @@ def tile_scaled_spectral_scores_g2_kernel(tc, spectra, loadings, gains, centers,
 
         every = range(PASSES)
         for c in every:
+            warm([2, 3, 0][c])
             prepare_x(0, c)
+            warm([0, 2, 0][c])
             if c > 0:
                 for t in range(PACK):
                     multiply(0, t, [c - 1])
             weave_p(0, c)
             quant_x(0, c)
             quant_p(0, c)
+        def one_pass(k, c):
+            for t in range(PACK):
+                multiply(k, t, [c])
+
+        def turn_pass(i, c):
+            turn_x(i, c, 0)
+            turn_x(i, c, 1)
+
+        def drain_pass(i, c):
+            drain_x(i, c, 0)
+            drain_x(i, c, 1)
+
         prepare_x(1, 0)
-        for t in range(PACK):
-            multiply(0, t, [PASSES - 1])
+        weave_p(1, 0)
+        one_pass(0, 2)
         prepare_x(1, 1)
+        quant_x(1, 0)
+        gain(0, 0)
+        gain(0, 1)
+        quant_p(1, 0)
         prepare_x(1, 2)
-        for t in range(PACK):
-            if t < PASSES:
-                quant_x(1, t)
-            gain(0, t)
-        for t in range(PACK):
-            multiply(1, t, every)
-        for t in range(PACK):
-            center(0, t)
-            if t < PASSES:
-                weave_p(1, t)
-            if t > 0:
-                quant_p(1, t - 1)
+        quant_x(1, 1)
+        gain(0, 2)
+        gain(0, 3)
+        one_pass(1, 0)
+        one_pass(1, 1)
+        quant_x(1, 2)
+        one_pass(1, 2)
+        center(0, 0)
+        weave_p(1, 1)
+        center(0, 1)
+        turn_pass(2, 0)
+        weave_p(1, 2)
+        quant_p(1, 1)
+        center(0, 2)
+        center(0, 3)
+        gain(1, 0)
+        quant_p(1, 2)
+        gain(1, 1)
+        gain(1, 2)
+        gain(1, 3)
+        drain_pass(2, 0)
+        one_pass(2, 0)
+        turn_pass(2, 1)
+        one_pass(2, 1)
+        one_pass(2, 2)
+        center(1, 0)
+        center(1, 1)
+        quant_x(2, 0)
+        weave_y_vector(0)
+        weave_y_scalar(0)
+        drain_pass(2, 1)
+        center(1, 2)
+        center(1, 3)
+        quant_y(0)
 
         last = len(UNITS) - 1
-        for k in range(1, last + 1):
-            ahead = (k + 3) // 2
-            halves = HALVES[3 * ((k + 1) % 2):3 * ((k + 1) % 2) + 3] if ahead < I else []
+        runs = {2: [(2, 2), None], 3: [(3, 0), (3, 1)], 4: [(3, 2), None]}
+        carry = (2, 1)
+        for k in range(2, last + 1):
+            r0, r1 = runs.get(k, [None, None])
             weave_y_scalar(k - 1)
-            for c, h in halves:
-                turn_x(ahead, c, h)
+            if r0:
+                turn_pass(*r0)
             for t in range(PACK):
                 gain(k, t)
                 center(k, t)
-                if t < len(halves):
-                    drain_x(ahead, *halves[t])
+                if carry and t == CARRY_AT:
+                    quant_x(*carry)
+                if r0 and t < 2:
+                    drain_x(r0[0], r0[1], t)
+                if r1 and t == 2:
+                    turn_pass(*r1)
                 if k < last:
                     multiply(k + 1, t, every)
-                if t == (1 if k < last else PACK - 1):
-                    weave_y_vector(k - 1)
-            whole = [c for c, h in halves if h == 1]
-            for c in whole[:1]:
-                quant_x(ahead, c)
+            weave_y_vector(k - 1)
+            if r0:
+                quant_x(*r0)
+            if r1:
+                drain_pass(*r1)
             quant_y(k - 1)
-            for c in whole[1:]:
-                quant_x(ahead, c)
+            carry = r1
             if k == last - 1:
                 store_scales(nc.sync, slice(0, (I - 1) * S))
         weave_y_vector(last)

from contextlib import ExitStack

import concourse.mybir as mybir
from concourse.masks import make_identity

I, S, W, C = 4, 512, 1536, 1024
FLOPS = 2 * C * I * S * W

F32 = mybir.dt.float32
BF16 = mybir.dt.bfloat16
U32 = mybir.dt.uint32
I32 = mybir.dt.int32
U8 = mybir.dt.uint8
FP8X4 = mybir.dt.float8_e4m3fn_x4
ACT = mybir.ActivationFunctionType
ALU = mybir.AluOpType

P = 128
PACK = 4
KP = P * PACK
PASSES = W // KP
GROUPS = C // KP
UNITS = [(0, 0), (1, 0), (0, 1), (1, 1), (2, 0), (2, 1), (3, 0), (3, 1)]
HALVES = [(c, h) for c in range(PASSES) for h in range(2)]
P_SPLIT = [[3, 3, 3], [3, 2, 2]]
CARRY_AT = 1
Y_SPLIT = [448, 448, 448, 448, 256, 256, 256, 336]


def tile_scaled_spectral_scores_g2_kernel(tc, spectra, loadings, gains, centers, spreads, out_0, out_1, out_2):
    nc = tc.nc
    with ExitStack() as ctx:
        sb = ctx.enter_context(tc.tile_pool(name="sb", bufs=1))
        ps = ctx.enter_context(tc.psum_pool(name="ps", bufs=1))
        ctx.enter_context(tc.manual_schedule())
        turns = {}

        def rotating(pool, kind, depth, shape, dtype, align=None):
            n = turns.get(kind, 0)
            turns[kind] = n + 1
            name = "%s%d" % (kind, n % depth)
            if align is None:
                return pool.tile(shape, dtype, name=name, tag=name)
            return pool.tile(shape, dtype, name=name, tag=name, align_bytes=align)

        ident = sb.tile([P, P], F32)
        make_identity(nc, ident[:])

        gain_rows = sb.tile([P, 16], BF16)
        nc.scalar.dma_start(out=gain_rows[:], in_=gains.rearrange("i (p j) -> (i p) j", j=16))
        cen = sb.tile([P, GROUPS, PACK * I], BF16)
        nc.scalar.dma_start(out=cen[:], in_=centers.rearrange("(g p t) i -> p g (t i)", g=GROUPS, t=PACK))
        spr = sb.tile([P, GROUPS, PACK], BF16)
        nc.scalar.dma_start(out=spr[:], in_=spreads.rearrange("(g p t) -> p g t", g=GROUPS, t=PACK))

        x_raw, p_raw = {}, {}

        def load_x(i, c):
            x_raw[i, c] = sb.tile([P, 4, KP], BF16, name="x_raw%d%d" % (i, c))
            nc.sync.dma_start(out=x_raw[i, c][:], in_=spectra[i, :, c * KP:(c + 1) * KP].rearrange("(j p) k -> p j k", p=P))

        def load_p(g, c):
            p_raw[g, c] = sb.tile([P, PACK, KP], BF16, name="p_raw%d%d" % (g, c))
            nc.sync.dma_start(out=p_raw[g, c][:], in_=loadings[c * KP:(c + 1) * KP, g * KP:(g + 1) * KP].rearrange("(p j) n -> p j n", j=PACK))

        for c in range(PASSES):
            load_x(0, c)
            load_p(0, c)
        load_x(1, 0)
        load_p(1, 0)
        load_x(1, 1)
        load_x(1, 2)
        load_p(1, 1)
        load_p(1, 2)
        for i in range(2, I):
            for c in range(PASSES):
                load_x(i, c)

        warm_in = sb.tile([P, 256 * PACK], BF16, align_bytes=64)
        nc.vector.memset(warm_in[:].bitcast(I32), 0)
        warm_codes = sb.tile([P, 256], U32, align_bytes=64)
        warm_scales = sb.tile([P, 256], U8, align_bytes=64)
        nc.vector.quantize_mx(out=warm_codes[:].bitcast(FP8X4), scales=warm_scales[:], in_=warm_in[:])
        warm_out = ps.tile([P, S], F32, name="acc3", tag="acc3")

        def warm(n):
            for rep in range(2 * n):
                nc.tensor.matmul_mx(out=warm_out[:, :256], lhsT=warm_codes[:, :P].bitcast(FP8X4), lhsT_scale=warm_scales[:, :P],
                                    rhs=warm_codes[:].bitcast(FP8X4), rhs_scale=warm_scales[:], start=True, stop=True)

        warm(2)
        gain_all = sb.tile([P, I * S], BF16)
        gain_words = gain_rows[:].bitcast(F32)
        gain_out = gain_all[:].bitcast(F32).rearrange("q (n w) -> q n w", w=8)
        for h in range(2):
            bank = rotating(ps, "xt", 4, [P, 4, P], F32)
            for w in range(4):
                nc.tensor.transpose(bank[:, w, :], gain_words[:, 4 * h + w:4 * h + w + 1].to_broadcast([P, P]), ident[:])
            nc.vector.tensor_copy(out=gain_out[:, :, 4 * h:4 * h + 4], in_=bank[:].rearrange("q w n -> q n w"))

        neg_cen = sb.tile([P, GROUPS * PACK, I], F32)
        nc.scalar.activation(out=neg_cen[:].rearrange("p j i -> p (j i)"), in_=cen[:].rearrange("p g f -> p (g f)"), func=ACT.Identity, scale=-1.0)
        inv = sb.tile([P, GROUPS * PACK], F32)
        nc.vector.reciprocal(out=inv[:], in_=spr[:].rearrange("p g t -> p (g t)"))
        shift = sb.tile([P, GROUPS * PACK, I], F32)
        nc.vector.tensor_tensor(out=shift[:], in0=neg_cen[:], in1=inv[:].unsqueeze(2).to_broadcast([P, GROUPS * PACK, I]), op=ALU.mult)

        x_bank, x_grp, x_codes, x_scales = {}, {}, {}, {}
        p_grp, p_codes, p_scales = {}, {}, {}
        acc, y, y_grp = {}, {}, {}
        y_scales = sb.tile([P, GROUPS, I * S], U8, align_bytes=64)

        def turn_x(i, c, h):
            words = x_raw[i, c][:].bitcast(F32)
            x_bank[i, c, h] = rotating(ps, "xt", 4, [P, 2, 2, P], F32)
            for j in range(2):
                for u in range(2):
                    nc.tensor.transpose(x_bank[i, c, h][:, j, u, :], words[:, 2 * h + j, u::2], ident[:])

        def drain_x(i, c, h):
            if h == 0:
                x_grp[i, c] = rotating(sb, "x_grp", 4, [P, S * PACK], BF16, 64)
            dst = x_grp[i, c][:].bitcast(F32)[:, h * 512:(h + 1) * 512].rearrange("p (j r u) -> p j r u", j=2, u=2)
            nc.scalar.copy(out=dst, in_=x_bank[i, c, h][:].rearrange("p j u r -> p j r u"))

        def quant_x(i, c):
            x_codes[i, c] = sb.tile([P, S], U32, name="x_codes%d%d" % (i, c), align_bytes=64)
            x_scales[i, c] = sb.tile([P, S], U8, name="x_scales%d%d" % (i, c), align_bytes=64)
            nc.vector.quantize_mx(out=x_codes[i, c][:].bitcast(FP8X4), scales=x_scales[i, c][:], in_=x_grp[i, c][:])

        def weave_p(g, c):
            p_grp[g, c] = rotating(sb, "p_grp", 4, [P, KP * PACK], BF16, 64)
            dst = p_grp[g, c][:].rearrange("p (t a b j) -> p a t b j", t=PACK, b=2, j=PACK)
            src = p_raw[g, c][:].rearrange("p j (a b t) -> p a t b j", b=2, t=PACK)
            cut = P_SPLIT[g][c]
            nc.vector.tensor_copy(out=dst[:, :, :cut], in_=src[:, :, :cut])
            nc.scalar.copy(out=dst[:, :, cut:], in_=src[:, :, cut:])

        def quant_p(g, c):
            p_codes[g, c] = sb.tile([P, KP], U32, name="p_codes%d%d" % (g, c), align_bytes=64)
            p_scales[g, c] = sb.tile([P, KP], U8, name="p_scales%d%d" % (g, c), align_bytes=64)
            nc.vector.quantize_mx(out=p_codes[g, c][:].bitcast(FP8X4), scales=p_scales[g, c][:], in_=p_grp[g, c][:])

        def multiply(k, t, passes):
            i, g = UNITS[k]
            if (k, t) not in acc:
                acc[k, t] = rotating(ps, "acc", 4, [P, S], F32)
            cols = slice(t * P, (t + 1) * P)
            for c in passes:
                nc.tensor.matmul_mx(
                    out=acc[k, t][:],
                    lhsT=p_codes[g, c][:, cols].bitcast(FP8X4), lhsT_scale=p_scales[g, c][:, cols],
                    rhs=x_codes[i, c][:].bitcast(FP8X4), rhs_scale=x_scales[i, c][:],
                    start=(c == 0), stop=(c == PASSES - 1))

        def gain(k, t):
            i, g = UNITS[k]
            if t == 0:
                y[k] = rotating(sb, "y", 6, [P, PACK, S], F32)
            nc.vector.tensor_tensor(out=y[k][:, t, :], in0=acc[k, t][:], in1=gain_all[:, i * S:(i + 1) * S], op=ALU.mult)

        def center(k, t):
            i, g = UNITS[k]
            j = g * PACK + t
            nc.scalar.activation(out=y[k][:, t, :], in_=y[k][:, t, :], func=ACT.Identity, scale=inv[:, j:j + 1], bias=shift[:, j, i:i + 1])
            rows = out_0[g * KP:(g + 1) * KP, i, :].rearrange("(p t) m -> p t m", t=PACK)
            nc.sync.dma_start(out=rows[:, t, :], in_=y[k][:, t, :])

        def weave_views(k):
            if k not in y_grp:
                y_grp[k] = rotating(sb, "y_grp", 2, [P, S * PACK], BF16, 64)
            dst = y_grp[k][:].rearrange("p (a b t) -> p a t b", b=4, t=PACK)
            src = y[k][:].rearrange("p t (a b) -> p a t b", b=4)
            return dst, src, Y_SPLIT[k] // 4

        def weave_y_vector(k):
            dst, src, cut = weave_views(k)
            nc.vector.tensor_copy(out=dst[:, :cut], in_=src[:, :cut])

        def weave_y_scalar(k):
            dst, src, cut = weave_views(k)
            nc.scalar.copy(out=dst[:, cut:], in_=src[:, cut:])

        def quant_y(k):
            i, g = UNITS[k]
            cols = slice(i * S, (i + 1) * S)
            y_codes = rotating(sb, "y_codes", 4, [P, S], U32, 64)
            nc.vector.quantize_mx(out=y_codes[:].bitcast(FP8X4), scales=y_scales[:, g, cols], in_=y_grp[k][:])
            nc.sync.dma_start(out=out_1[g, :, cols, :].rearrange("p m t -> p (m t)").bitcast(I32), in_=y_codes[:].bitcast(I32))

        def store_scales(engine, cols):
            for q in range(4):
                engine.dma_start(out=out_2[:, 4 * q:4 * q + 4, cols].rearrange("g r n -> r g n").bitcast(I32),
                                 in_=y_scales[32 * q:32 * q + 4, :, cols].bitcast(I32))

        def prepare_x(i, c):
            for h in range(2):
                turn_x(i, c, h)
                drain_x(i, c, h)

        every = range(PASSES)
        for c in every:
            warm([2, 3, 0][c])
            prepare_x(0, c)
            warm([0, 2, 0][c])
            if c > 0:
                for t in range(PACK):
                    multiply(0, t, [c - 1])
            weave_p(0, c)
            quant_x(0, c)
            quant_p(0, c)
        def one_pass(k, c):
            for t in range(PACK):
                multiply(k, t, [c])

        def turn_pass(i, c):
            turn_x(i, c, 0)
            turn_x(i, c, 1)

        def drain_pass(i, c):
            drain_x(i, c, 0)
            drain_x(i, c, 1)

        prepare_x(1, 0)
        weave_p(1, 0)
        one_pass(0, 2)
        prepare_x(1, 1)
        quant_x(1, 0)
        gain(0, 0)
        gain(0, 1)
        quant_p(1, 0)
        prepare_x(1, 2)
        quant_x(1, 1)
        gain(0, 2)
        gain(0, 3)
        one_pass(1, 0)
        one_pass(1, 1)
        quant_x(1, 2)
        one_pass(1, 2)
        center(0, 0)
        weave_p(1, 1)
        center(0, 1)
        turn_pass(2, 0)
        weave_p(1, 2)
        quant_p(1, 1)
        center(0, 2)
        center(0, 3)
        gain(1, 0)
        quant_p(1, 2)
        gain(1, 1)
        gain(1, 2)
        gain(1, 3)
        drain_pass(2, 0)
        one_pass(2, 0)
        turn_pass(2, 1)
        one_pass(2, 1)
        one_pass(2, 2)
        center(1, 0)
        center(1, 1)
        quant_x(2, 0)
        weave_y_vector(0)
        weave_y_scalar(0)
        drain_pass(2, 1)
        center(1, 2)
        center(1, 3)
        quant_y(0)

        last = len(UNITS) - 1
        runs = {2: [(2, 2), None], 3: [(3, 0), (3, 1)], 4: [(3, 2), None]}
        carry = (2, 1)
        for k in range(2, last + 1):
            r0, r1 = runs.get(k, [None, None])
            weave_y_scalar(k - 1)
            if r0:
                turn_pass(*r0)
            for t in range(PACK):
                gain(k, t)
                center(k, t)
                if carry and t == CARRY_AT:
                    quant_x(*carry)
                if r0 and t < 2:
                    drain_x(r0[0], r0[1], t)
                if r1 and t == 2:
                    turn_pass(*r1)
                if k < last:
                    multiply(k + 1, t, every)
            weave_y_vector(k - 1)
            if r0:
                quant_x(*r0)
            if r1:
                drain_pass(*r1)
            quant_y(k - 1)
            carry = r1
            if k == last - 1:
                store_scales(nc.sync, slice(0, (I - 1) * S))
        weave_y_vector(last)
        weave_y_scalar(last)
        quant_y(last)
        store_scales(nc.scalar, slice((I - 1) * S, I * S))
